import numpy as np
import ml_dtypes


def mxq(x, axis, fmt="e4m3"):
    dtype, down = {"e4m3": (ml_dtypes.float8_e4m3fn, 7), "e5m2": (ml_dtypes.float8_e5m2, 14)}[fmt]
    v = np.moveaxis(np.asarray(x, np.float32).astype(ml_dtypes.bfloat16).astype(np.float64), axis, -1)
    blocks = v.reshape(v.shape[:-1] + (-1, 32))
    amax = np.abs(blocks).max(-1, keepdims=True)
    byte = np.maximum(np.where(amax > 0, np.frexp(amax)[1] - 1 + 127, 0) - down, 1)
    scale = np.exp2(byte - 127.0)
    codes = (blocks / scale).astype(np.float32).astype(dtype).astype(np.float64)
    return np.moveaxis((codes * scale).reshape(v.shape), -1, axis)


WIDE = False


def mx_kscale(k):
    if not WIDE:
        return np.ones(k)
    levels = np.array([30, -30])
    if k % 512:
        return np.exp2(np.random.permutation(np.resize(levels, k // 32))).repeat(32)
    a = np.empty((k // 512, 16))
    for p in range(k // 512):
        a[p, :8] = np.random.permutation(np.resize(levels, 8))
        for g in range(8):
            far = levels[np.abs(levels - a[p, g]) >= 10]
            a[p, g + 8] = far[np.random.randint(len(far))]
    return np.exp2(a.ravel()).repeat(32)


def f64(x):
    return np.asarray(x).astype(np.float64)


def striped(idx):
    return np.tile(np.asarray(idx).reshape(-1, 16).T, (8, 1)).astype(np.uint16)


def unstriped(offs):
    return offs[:16].T.reshape(-1).astype(np.int64)


E2M1 = np.array([0.0, 0.5, 1.0, 1.5, 2.0, 3.0, 4.0, 6.0, -0.0, -0.5, -1.0, -1.5, -2.0, -3.0, -4.0, -6.0])


def pack_weight(w, fmt):
    k, n = w.shape
    w = f64(np.asarray(w, np.float32).astype(ml_dtypes.bfloat16)).reshape(k // 32, 32, n)
    amax = np.abs(w).max(1)
    if fmt in ("e4m3", "e5m2"):
        byte = np.frexp(amax)[1] - 1 + 127 - (7 if fmt == "e4m3" else 14)
    else:
        mant, ex = np.frexp(amax / 6.0)
        byte = np.where(mant > 0.5, ex, ex - 1) + 127
    byte = np.clip(np.where(amax > 0, byte, 1), 1, 254)
    scaled = (w * np.exp2(127.0 - byte)[:, None, :]).reshape(k, n).astype(np.float32)
    by_word = np.ascontiguousarray(scaled.reshape(k // 512, 128, 4, n).transpose(0, 1, 3, 2))
    if fmt in ("e4m3", "e5m2"):
        words = by_word.astype(ml_dtypes.float8_e4m3fn if fmt == "e4m3" else ml_dtypes.float8_e5m2).view(np.uint8)
    else:
        c = by_word.astype(ml_dtypes.float4_e2m1fn).view(np.uint8) & 0xF
        words = (c[..., 0::2] | (c[..., 1::2] << 4)).reshape(k // 512, 128, 2 * n)
    return np.ascontiguousarray(words), np.ascontiguousarray(byte.astype(np.uint8).reshape(k // 512, 16, n))


def unpack_weight(words, scales, fmt):
    g, _, n = scales.shape
    words = np.ascontiguousarray(words).reshape(g, 128, n, -1)
    if fmt in ("e4m3", "e5m2"):
        vals = words.view(ml_dtypes.float8_e4m3fn if fmt == "e4m3" else ml_dtypes.float8_e5m2).astype(np.float64)
    else:
        nib = np.empty((g, 128, n, 4), np.uint8)
        nib[..., 0::2] = words & 0xF
        nib[..., 1::2] = words >> 4
        vals = E2M1[nib]
    vals = vals * np.repeat(np.exp2(scales.astype(np.float64) - 127.0), 8, axis=1)[..., None]
    return vals.transpose(0, 1, 3, 2).reshape(g * 512, n)


K, F, T, Z, J, R, C, O, N, E = 512, 512, 1024, 1024, 256, 512, 512, 128, 256, 1024


def setup_inputs():
    n = np.random.standard_normal
    idx = np.random.permutation(T)[:J]
    idx2 = np.random.permutation(Z)[:J]
    idx3 = np.random.permutation(C)[:J]
    idx4 = np.random.permutation(C)[:O]
    idx5 = np.random.permutation(C)[:O]
    idx6 = np.random.permutation(J)[:O]
    idx7 = np.random.permutation(E)[:O]
    fk = mx_kscale(K)
    fr = mx_kscale(R)
    ff = mx_kscale(F)
    xtp = pack_weight(n((K, T)) / fk[:, None], "e5m2")
    wp = pack_weight(n((K, R)) * 1 / np.sqrt(K) * fk[:, None] * fr, "e2m1")
    xop = pack_weight(n((F, Z)) / ff[:, None], "e4m3")
    w2p = pack_weight(n((F, R)) * 1 / np.sqrt(F) * ff[:, None] * fr, "e2m1")
    wbp = pack_weight(n((R, N)) * 1 / np.sqrt(R) / fr[:, None], "e2m1")
    return {
        "xt_words": xtp[0],
        "xt_scales": xtp[1],
        "w_words": wp[0],
        "w_scales": wp[1],
        "xo_words": xop[0],
        "xo_scales": xop[1],
        "w2_words": w2p[0],
        "w2_scales": w2p[1],
        "wb_words": wbp[0],
        "wb_scales": wbp[1],
        "tz": (n((N, E))).astype(np.float32),
        "offs": striped(idx),
        "offs2": striped(idx2),
        "offs3": striped(idx3),
        "offs4": striped(idx4),
        "offs5": striped(idx5),
        "offs6": striped(idx6),
        "offs7": striped(idx7),
    }


def reference(xt_words, xt_scales, w_words, w_scales, xo_words, xo_scales, w2_words, w2_scales, wb_words, wb_scales, tz, offs, offs2, offs3, offs4, offs5, offs6, offs7):
    idx = unstriped(offs)
    idx2 = unstriped(offs2)
    idx3 = unstriped(offs3)
    idx4 = unstriped(offs4)
    idx5 = unstriped(offs5)
    idx6 = unstriped(offs6)
    idx7 = unstriped(offs7)
    xtu = unpack_weight(xt_words, xt_scales, "e5m2")
    wu = unpack_weight(w_words, w_scales, "e2m1")
    xou = unpack_weight(xo_words, xo_scales, "e4m3")
    w2u = unpack_weight(w2_words, w2_scales, "e2m1")
    wbu = unpack_weight(wb_words, wb_scales, "e2m1")
    xtidxg = xtu[:, idx]
    a = wu.T @ xtidxg
    xoidx2g = xou[:, idx2]
    b = w2u.T @ xoidx2g
    pw = np.zeros((R, C))
    pw[:, idx3] = a
    hid = np.maximum(pw[:, idx4], pw[:, idx5]) - b[:, idx6]
    hidq = mxq(hid, 0, "e4m3")
    p = wbu.T @ hidq
    y = p + f64(tz)[:, idx7]
    return y

@@ -1,0 +1,169 @@
+from contextlib import ExitStack
+
+import concourse.mybir as mybir
+
+F32 = mybir.dt.float32
+BF16 = mybir.dt.bfloat16
+I32 = mybir.dt.int32
+U32 = mybir.dt.uint32
+U16 = mybir.dt.uint16
+U8 = mybir.dt.uint8
+E4M3 = mybir.dt.float8_e4m3fn_x4
+E5M2 = mybir.dt.float8_e5m2_x4
+E2M1 = mybir.dt.float4_e2m1fn_x4
+ALU = mybir.AluOpType
+COPY = mybir.ActivationFunctionType.Copy
+
+P = 128
+PACK = 4
+T, Z, J, R, C, O, N, E = 1024, 1024, 256, 512, 512, 128, 256, 1024
+FLOPS = 301989888
+
+
+def tile_list_readless_twotab_one_tabled_kernel(tc, xt_words, xt_scales, w_words, w_scales, xo_words, xo_scales,
+                                                     w2_words, w2_scales, wb_words, wb_scales, tz,
+                                                     offs, offs2, offs3, offs4, offs5, offs6, offs7, out):
+    nc = tc.nc
+    with ExitStack() as ctx:
+        sb = ctx.enter_context(tc.tile_pool(name="sb", bufs=1))
+        psum = ctx.enter_context(tc.psum_pool(name="psum", bufs=1))
+
+        def tile(name, shape, dtype):
+            return sb.tile(shape, dtype, name=name, align_bytes=64)
+
+        def load_list(name, src):
+            t = tile(name, [P, src.shape[1]], U16)
+            nc.sync.dma_start(t[:], src)
+            return t
+
+        def load_words(name, src, dtype, cols, queue):
+            t = tile(name, [P, cols], dtype)
+            queue.dma_start(t[:].bitcast(I32), src.bitcast(I32))
+            return t
+
+        def plane_head(t, src, queue):
+            queue.dma_start(t[0:2, :].bitcast(I32), src[0, 0:2, :].bitcast(I32))
+
+        def plane_rest(t, src, queue):
+            rows = src[0, 2:16, :].bitcast(I32)
+            queue.dma_start(t[2:P, :].bitcast(I32), rows.unsqueeze(0).broadcast_to([9, 14, src.shape[2] // 4]))
+
+        xt_s = tile("xt_s", [P, T], U8)
+        w_s = tile("w_s", [P, R], U8)
+        xo_s = tile("xo_s", [P, Z], U8)
+        w2_s = tile("w2_s", [P, R], U8)
+        wb_s = tile("wb_s", [P, N], U8)
+        tzt = tile("tzt", [P, 2, E], F32)
+        pw = [tile("pw%d" % t, [P, C], F32) for t in range(PACK)]
+        for t in range(PACK):
+            nc.vector.memset(pw[t][:], 0.0)
+
+        plane_head(xt_s, xt_scales, nc.scalar)
+        xt_w = load_words("xt_w", xt_words[0].rearrange("p c t -> p (c t)"), U32, T, nc.sync)
+        plane_rest(w_s, w_scales, nc.sync)
+        plane_rest(xt_s, xt_scales, nc.scalar)
+        plane_rest(xo_s, xo_scales, nc.gpsimd)
+        plane_rest(w2_s, w2_scales, nc.gpsimd)
+        l1 = load_list("l1", offs)
+        plane_head(w_s, w_scales, nc.scalar)
+        w_w = load_words("w_w", w_words[0], U8, 2 * R, nc.scalar)
+        l3 = load_list("l3", offs3)
+        xo_w = load_words("xo_w", xo_words[0].rearrange("p c t -> p (c t)"), U32, Z, nc.sync)
+        l2 = load_list("l2", offs2)
+        plane_head(xo_s, xo_scales, nc.sync)
+        w2_w = load_words("w2_w", w2_words[0], U8, 2 * R, nc.sync)
+        plane_head(w2_s, w2_scales, nc.sync)
+        l4 = load_list("l4", offs4)
+        l5 = load_list("l5", offs5)
+        l6 = load_list("l6", offs6)
+        nc.sync.dma_start(tzt[:], tz.rearrange("(h p) e -> p h e", p=P))
+        l7 = load_list("l7", offs7)
+        wb_w = load_words("wb_w", wb_words[0], U8, 2 * N, nc.sync)
+        plane_head(wb_s, wb_scales, nc.sync)
+        plane_rest(wb_s, wb_scales, nc.sync)
+
+        def deal_words(name, src):
+            t = tile(name, [P, 2 * R], U8)
+            nc.scalar.copy(t[:].bitcast(U16).rearrange("p (t m) -> p t m", t=PACK),
+                           src[:].bitcast(U16).rearrange("p (m t) -> p t m", t=PACK))
+            return t
+
+        def deal_plane(name, src, eng):
+            t = tile(name, [P, R], U8)
+            eng.tensor_copy(t[:].rearrange("p (t m) -> p t m", t=PACK), src[:].rearrange("p (m t) -> p t m", t=PACK))
+            return t
+
+        def gather_packed(name, src, lst, dtype):
+            t = tile(name, [P, J], dtype)
+            nc.vector.tensor_copy(t[:], src[:].indirect(lst[:]))
+            return t
+
+        def first_product(bank, t, ww, ws, xw, xs, fmt):
+            nc.tensor.matmul_mx(out=bank, lhsT=ww[:, 2 * P * t : 2 * P * (t + 1)].bitcast(E2M1),
+                                lhsT_scale=ws[:, P * t : P * (t + 1)], rhs=xw[:].bitcast(fmt), rhs_scale=xs[:],
+                                start=True, stop=True)
+
+        w_wd = deal_words("w_wd", w_w)
+        xt_wg = gather_packed("xt_wg", xt_w, l1, U32)
+        xt_sg = gather_packed("xt_sg", xt_s, l1, U8)
+        w_sd = deal_plane("w_sd", w_s, nc.gpsimd)
+        a_ps = [psum.tile([P, J], F32, name="a_ps%d" % t) for t in range(PACK)]
+        a_sb = [tile("a_sb%d" % t, [P, J], F32) for t in range(PACK)]
+        for t in range(PACK):
+            first_product(a_ps[t][:], t, w_wd, w_sd, xt_wg, xt_sg, E5M2)
+
+        def put_scalar(t):
+            nc.scalar.copy(a_sb[t][:], a_ps[t][:])
+            nc.scalar.activation(pw[t][:].indirect(l3[:]), a_sb[t][:], COPY)
+
+        def put_vector(t):
+            nc.vector.tensor_copy(a_sb[t][:], a_ps[t][:])
+            nc.vector.tensor_copy(pw[t][:].indirect(l3[:]), a_sb[t][:])
+
+        put_scalar(0)
+        put_vector(1)
+        w2_wd = deal_words("w2_wd", w2_w)
+        put_scalar(2)
+        xo_wg = gather_packed("xo_wg", xo_w, l2, U32)
+        xo_sg = gather_packed("xo_sg", xo_s, l2, U8)
+        w2_sd = deal_plane("w2_sd", w2_s, nc.gpsimd)
+        put_vector(3)
+
+        b_ps = [psum.tile([P, 2, J], F32, name="b_ps%d" % u) for u in range(2)]
+        b_sb = [tile("b_sb%d" % u, [P, 2, J], F32) for u in range(2)]
+        for t in range(PACK):
+            first_product(b_ps[t // 2][:, t % 2, :], t, w2_wd, w2_sd, xo_wg, xo_sg, E4M3)
+        g4 = tile("g4", [P, PACK, O], F32)
+        g5 = tile("g5", [P, PACK, O], F32)
+        bg = tile("bg", [P, PACK, O], F32)
+        for u in range(2):
+            nc.scalar.copy(b_sb[u][:], b_ps[u][:])
+        for t in range(PACK):
+            nc.scalar.activation(bg[:, t, :], b_sb[t // 2][:, t % 2, :].indirect(l6[:]), COPY)
+        for t in range(PACK):
+            nc.vector.tensor_copy(g4[:, t, :], pw[t][:].indirect(l4[:]))
+            if t < 2:
+                nc.vector.tensor_copy(g5[:, t, :], pw[t][:].indirect(l5[:]))
+            else:
+                nc.scalar.activation(g5[:, t, :], pw[t][:].indirect(l5[:]), COPY)
+        tzg = tile("tzg", [P, 2, O], F32)
+        for h in range(2):
+            nc.scalar.activation(tzg[:, h, :], tzt[:, h, :].indirect(l7[:]), COPY)
+
+        top = tile("top", [P, PACK, O], F32)
+        nc.vector.tensor_tensor(top[:], g4[:], g5[:], ALU.max)
+        hid = tile("hid", [P, O * PACK], BF16)
+        nc.vector.tensor_tensor(hid[:].rearrange("p (c i t) -> p c t i", i=4, t=PACK),
+                                top[:].rearrange("p t (c i) -> p c t i", i=4),
+                                bg[:].rearrange("p t (c i) -> p c t i", i=4), ALU.subtract)
+        hid_w = tile("hid_w", [P, O], U32)
+        hid_s = tile("hid_s", [P, O], U8)
+        nc.vector.quantize_mx(out=hid_w[:].bitcast(E4M3), scales=hid_s[:], in_=hid[:])
+        p_ps = psum.tile([P, 2, O], F32, name="p_ps")
+        for h in range(2):
+            nc.tensor.matmul_mx(out=p_ps[:, h, :], lhsT=wb_w[:, 2 * P * h : 2 * P * (h + 1)].bitcast(E2M1),
+                                lhsT_scale=wb_s[:, P * h : P * (h + 1)], rhs=hid_w[:].bitcast(E4M3), rhs_scale=hid_s[:],
+                                start=True, stop=True)
+        res = tile("res", [P, 2, O], F32)
+        nc.vector.tensor_tensor(res[:], p_ps[:], tzg[:], ALU.add)
+        nc.sync.dma_start(out.rearrange("(h p) o -> p h o", p=P), res[:])

@@ -28,8 +28,8 @@ def tile_list_readless_twotab_one_tabled_kernel(tc, xt_words, xt_scales, w_words
         sb = ctx.enter_context(tc.tile_pool(name="sb", bufs=1))
         psum = ctx.enter_context(tc.psum_pool(name="psum", bufs=1))
 
-        def tile(name, shape, dtype):
-            return sb.tile(shape, dtype, name=name, align_bytes=64)
+        def tile(name, shape, dtype, slot=None):
+            return sb.tile(shape, dtype, name=name, tag=slot or name, align_bytes=64)
 
         def load_list(name, src):
             t = tile(name, [P, src.shape[1]], U16)
@@ -40,6 +40,9 @@ def tile_list_readless_twotab_one_tabled_kernel(tc, xt_words, xt_scales, w_words
             t = tile(name, [P, cols], dtype)
             queue.dma_start(t[:].bitcast(I32), src.bitcast(I32))
             return t
+
+        def plane_quadrant(t, src, q, queue):
+            queue.dma_start(t[32 * q : 32 * q + 4, :].bitcast(I32), src[0, 4 * q : 4 * q + 4, :].bitcast(I32))
 
         def plane_head(t, src, queue):
             queue.dma_start(t[0:2, :].bitcast(I32), src[0, 0:2, :].bitcast(I32))
@@ -55,24 +58,25 @@ def tile_list_readless_twotab_one_tabled_kernel(tc, xt_words, xt_scales, w_words
         wb_s = tile("wb_s", [P, N], U8)
         tzt = tile("tzt", [P, 2, E], F32)
         pw = [tile("pw%d" % t, [P, C], F32) for t in range(PACK)]
+        nc.vector.memset(xt_s[:].bitcast(I32), 0)
         for t in range(PACK):
             nc.vector.memset(pw[t][:], 0.0)
 
-        plane_head(xt_s, xt_scales, nc.scalar)
+        l1 = load_list("l1", offs)
         xt_w = load_words("xt_w", xt_words[0].rearrange("p c t -> p (c t)"), U32, T, nc.sync)
         plane_rest(w_s, w_scales, nc.sync)
-        plane_rest(xt_s, xt_scales, nc.scalar)
+        plane_head(w_s, w_scales, nc.gpsimd)
         plane_rest(xo_s, xo_scales, nc.gpsimd)
-        plane_rest(w2_s, w2_scales, nc.gpsimd)
-        l1 = load_list("l1", offs)
-        plane_head(w_s, w_scales, nc.scalar)
-        w_w = load_words("w_w", w_words[0], U8, 2 * R, nc.scalar)
-        l3 = load_list("l3", offs3)
+        w_w = load_words("w_w", w_words[0], U8, 2 * R, nc.sync)
+        for q in range(4):
+            plane_quadrant(xt_s, xt_scales, q, nc.scalar)
         xo_w = load_words("xo_w", xo_words[0].rearrange("p c t -> p (c t)"), U32, Z, nc.sync)
         l2 = load_list("l2", offs2)
         plane_head(xo_s, xo_scales, nc.sync)
+        l3 = load_list("l3", offs3)
         w2_w = load_words("w2_w", w2_words[0], U8, 2 * R, nc.sync)
         plane_head(w2_s, w2_scales, nc.sync)
+        plane_rest(w2_s, w2_scales, nc.sync)
         l4 = load_list("l4", offs4)
         l5 = load_list("l5", offs5)
         l6 = load_list("l6", offs6)
@@ -82,15 +86,9 @@ def tile_list_readless_twotab_one_tabled_kernel(tc, xt_words, xt_scales, w_words
         plane_head(wb_s, wb_scales, nc.sync)
         plane_rest(wb_s, wb_scales, nc.sync)
 
-        def deal_words(name, src):
-            t = tile(name, [P, 2 * R], U8)
-            nc.scalar.copy(t[:].bitcast(U16).rearrange("p (t m) -> p t m", t=PACK),
-                           src[:].bitcast(U16).rearrange("p (m t) -> p t m", t=PACK))
-            return t
-
-        def deal_plane(name, src, eng):
+        def deal_plane(name, src):
             t = tile(name, [P, R], U8)
-            eng.tensor_copy(t[:].rearrange("p (t m) -> p t m", t=PACK), src[:].rearrange("p (m t) -> p t m", t=PACK))
+            nc.gpsimd.tensor_copy(t[:].rearrange("p (t m) -> p t m", t=PACK), src[:].rearrange("p (m t) -> p t m", t=PACK))
             return t
 
         def gather_packed(name, src, lst, dtype):
@@ -103,31 +101,31 @@ def tile_list_readless_twotab_one_tabled_kernel(tc, xt_words, xt_scales, w_words
                                 lhsT_scale=ws[:, P * t : P * (t + 1)], rhs=xw[:].bitcast(fmt), rhs_scale=xs[:],
                                 start=True, stop=True)
 
-        w_wd = deal_words("w_wd", w_w)
+        w_wd = tile("w_wd", [P, 2 * R], U8)
+        nc.scalar.copy(w_wd[:].bitcast(U16).rearrange("p (t m) -> p t m", t=PACK),
+                       w_w[:].bitcast(U16).rearrange("p (m t) -> p t m", t=PACK))
         xt_wg = gather_packed("xt_wg", xt_w, l1, U32)
         xt_sg = gather_packed("xt_sg", xt_s, l1, U8)
-        w_sd = deal_plane("w_sd", w_s, nc.gpsimd)
-        a_ps = [psum.tile([P, J], F32, name="a_ps%d" % t) for t in range(PACK)]
-        a_sb = [tile("a_sb%d" % t, [P, J], F32) for t in range(PACK)]
-        for t in range(PACK):
-            first_product(a_ps[t][:], t, w_wd, w_sd, xt_wg, xt_sg, E5M2)
-
-        def put_scalar(t):
-            nc.scalar.copy(a_sb[t][:], a_ps[t][:])
-            nc.scalar.activation(pw[t][:].indirect(l3[:]), a_sb[t][:], COPY)
-
-        def put_vector(t):
-            nc.vector.tensor_copy(a_sb[t][:], a_ps[t][:])
-            nc.vector.tensor_copy(pw[t][:].indirect(l3[:]), a_sb[t][:])
-
-        put_scalar(0)
-        put_vector(1)
-        w2_wd = deal_words("w2_wd", w2_w)
-        put_scalar(2)
         xo_wg = gather_packed("xo_wg", xo_w, l2, U32)
         xo_sg = gather_packed("xo_sg", xo_s, l2, U8)
-        w2_sd = deal_plane("w2_sd", w2_s, nc.gpsimd)
-        put_vector(3)
+        w_sd = deal_plane("w_sd", w_s)
+        w2_wd = tile("w2_wd", [P, 2 * R], U8)
+        nc.gpsimd.tensor_copy(w2_wd[:].rearrange("p (t m b) -> p t m b", t=PACK, b=2),
+                              w2_w[:].rearrange("p (m t b) -> p t m b", t=PACK, b=2))
+        w2_sd = deal_plane("w2_sd", w2_s)
+        a_ps = [psum.tile([P, J], F32, name="a_ps%d" % t) for t in range(PACK)]
+        a_sb = [tile("a_sb0", [P, J], F32), tile("a_sb1", [P, J], F32),
+                tile("a_sb2", [P, J], F32, slot="xo_s"), tile("a_sb3", [P, J], F32, slot="xo_w")]
+        for t in range(PACK):
+            first_product(a_ps[t][:], t, w_wd, w_sd, xt_wg, xt_sg, E5M2)
+        for t in (0, 1):
+            nc.scalar.copy(a_sb[t][:], a_ps[t][:])
+        for t in (2, 3):
+            nc.vector.tensor_copy(a_sb[t][:], a_ps[t][:])
+        for t in (0, 1):
+            nc.scalar.activation(pw[t][:].indirect(l3[:]), a_sb[t][:], COPY)
+        for t in (2, 3):
+            nc.vector.tensor_copy(pw[t][:].indirect(l3[:]), a_sb[t][:])
 
         b_ps = [psum.tile([P, 2, J], F32, name="b_ps%d" % u) for u in range(2)]
         b_sb = [tile("b_sb%d" % u, [P, 2, J], F32) for u in range(2)]
@@ -138,32 +136,36 @@ def tile_list_readless_twotab_one_tabled_kernel(tc, xt_words, xt_scales, w_words
         bg = tile("bg", [P, PACK, O], F32)
         for u in range(2):
             nc.scalar.copy(b_sb[u][:], b_ps[u][:])
+        for t in (0, 1):
+            nc.scalar.activation(g5[:, t, :], pw[t][:].indirect(l5[:]), COPY)
         for t in range(PACK):
             nc.scalar.activation(bg[:, t, :], b_sb[t // 2][:, t % 2, :].indirect(l6[:]), COPY)
         for t in range(PACK):
             nc.vector.tensor_copy(g4[:, t, :], pw[t][:].indirect(l4[:]))
-            if t < 2:
-                nc.vector.tensor_copy(g5[:, t, :], pw[t][:].indirect(l5[:]))
-            else:
-                nc.scalar.activation(g5[:, t, :], pw[t][:].indirect(l5[:]), COPY)
-        tzg = tile("tzg", [P, 2, O], F32)
+        for t in (2, 3):
+            nc.vector.tensor_copy(g5[:, t, :], pw[t][:].indirect(l5[:]))
+        tzg = tile("tzg", [P, 2, O], F32, slot="b_sb1")
         for h in range(2):
             nc.scalar.activation(tzg[:, h, :], tzt[:, h, :].indirect(l7[:]), COPY)
 
         top = tile("top", [P, PACK, O], F32)
-        nc.vector.tensor_tensor(top[:], g4[:], g5[:], ALU.max)
         hid = tile("hid", [P, O * PACK], BF16)
-        nc.vector.tensor_tensor(hid[:].rearrange("p (c i t) -> p c t i", i=4, t=PACK),
-                                top[:].rearrange("p t (c i) -> p c t i", i=4),
-                                bg[:].rearrange("p t (c i) -> p c t i", i=4), ALU.subtract)
         hid_w = tile("hid_w", [P, O], U32)
         hid_s = tile("hid_s", [P, O], U8)
-        nc.vector.quantize_mx(out=hid_w[:].bitcast(E4M3), scales=hid_s[:], in_=hid[:])
-        p_ps = psum.tile([P, 2, O], F32, name="p_ps")
+        halves = [slice(0, O // 2), slice(O // 2, O)]
+        for o in halves:
+            nc.vector.tensor_tensor(top[:, :, o], g4[:, :, o], g5[:, :, o], ALU.max)
+        for o in halves:
+            nc.vector.tensor_tensor(hid[:, PACK * o.start : PACK * o.stop].rearrange("p (c i t) -> p c t i", i=4, t=PACK),
+                                    top[:, :, o].rearrange("p t (c i) -> p c t i", i=4),
+                                    bg[:, :, o].rearrange("p t (c i) -> p c t i", i=4), ALU.subtract)
+        for o in halves:
+            nc.vector.quantize_mx(out=hid_w[:, o].bitcast(E4M3), scales=hid_s[:, o], in_=hid[:, PACK * o.start : PACK * o.stop])
         for h in range(2):
-            nc.tensor.matmul_mx(out=p_ps[:, h, :], lhsT=wb_w[:, 2 * P * h : 2 * P * (h + 1)].bitcast(E2M1),
+            p_ps = psum.tile([P, O], F32, name="p_ps%d" % h)
+            nc.tensor.matmul_mx(out=p_ps[:], lhsT=wb_w[:, 2 * P * h : 2 * P * (h + 1)].bitcast(E2M1),
                                 lhsT_scale=wb_s[:, P * h : P * (h + 1)], rhs=hid_w[:].bitcast(E4M3), rhs_scale=hid_s[:],
                                 start=True, stop=True)
-        res = tile("res", [P, 2, O], F32)
-        nc.vector.tensor_tensor(res[:], p_ps[:], tzg[:], ALU.add)
-        nc.sync.dma_start(out.rearrange("(h p) o -> p h o", p=P), res[:])
+            res = tile("res%d" % h, [P, O], F32)
+            nc.vector.tensor_tensor(res[:], p_ps[:], tzg[:, h, :], ALU.add)
+            (nc.sync if h == 0 else nc.scalar).dma_start(out[P * h : P * (h + 1), :], res[:])

@@ -58,27 +58,26 @@ def tile_list_readless_twotab_one_tabled_kernel(tc, xt_words, xt_scales, w_words
         wb_s = tile("wb_s", [P, N], U8)
         tzt = tile("tzt", [P, 2, E], F32)
         pw = [tile("pw%d" % t, [P, C], F32) for t in range(PACK)]
-        nc.vector.memset(xt_s[:].bitcast(I32), 0)
         for t in range(PACK):
-            nc.vector.memset(pw[t][:], 0.0)
+            nc.gpsimd.memset(pw[t][:], 0.0)
 
+        plane_head(xt_s, xt_scales, nc.scalar)
         l1 = load_list("l1", offs)
         xt_w = load_words("xt_w", xt_words[0].rearrange("p c t -> p (c t)"), U32, T, nc.sync)
+        plane_rest(xt_s, xt_scales, nc.scalar)
+        w_w = load_words("w_w", w_words[0], U8, 2 * R, nc.scalar)
+        plane_head(w_s, w_scales, nc.sync)
         plane_rest(w_s, w_scales, nc.sync)
-        plane_head(w_s, w_scales, nc.gpsimd)
-        plane_rest(xo_s, xo_scales, nc.gpsimd)
-        w_w = load_words("w_w", w_words[0], U8, 2 * R, nc.sync)
-        for q in range(4):
-            plane_quadrant(xt_s, xt_scales, q, nc.scalar)
         xo_w = load_words("xo_w", xo_words[0].rearrange("p c t -> p (c t)"), U32, Z, nc.sync)
         l2 = load_list("l2", offs2)
+        plane_rest(xo_s, xo_scales, nc.sync)
         plane_head(xo_s, xo_scales, nc.sync)
         l3 = load_list("l3", offs3)
-        w2_w = load_words("w2_w", w2_words[0], U8, 2 * R, nc.sync)
-        plane_head(w2_s, w2_scales, nc.sync)
         plane_rest(w2_s, w2_scales, nc.sync)
-        l4 = load_list("l4", offs4)
+        plane_head(w2_s, w2_scales, nc.sync)
+        w2_w = load_words("w2_w", w2_words[0], U8, 2 * R, nc.sync)
         l5 = load_list("l5", offs5)
+        l4 = load_list("l4", offs4)
         l6 = load_list("l6", offs6)
         nc.sync.dma_start(tzt[:], tz.rearrange("(h p) e -> p h e", p=P))
         l7 = load_list("l7", offs7)
@@ -88,11 +87,11 @@ def tile_list_readless_twotab_one_tabled_kernel(tc, xt_words, xt_scales, w_words
 
         def deal_plane(name, src):
             t = tile(name, [P, R], U8)
-            nc.gpsimd.tensor_copy(t[:].rearrange("p (t m) -> p t m", t=PACK), src[:].rearrange("p (m t) -> p t m", t=PACK))
+            nc.vector.tensor_copy(t[:].rearrange("p (t m) -> p t m", t=PACK), src[:].rearrange("p (m t) -> p t m", t=PACK))
             return t
 
-        def gather_packed(name, src, lst, dtype):
-            t = tile(name, [P, J], dtype)
+        def gather_packed(name, src, lst, dtype, slot=None):
+            t = tile(name, [P, J], dtype, slot)
             nc.vector.tensor_copy(t[:], src[:].indirect(lst[:]))
             return t
 
@@ -105,27 +104,27 @@ def tile_list_readless_twotab_one_tabled_kernel(tc, xt_words, xt_scales, w_words
         nc.scalar.copy(w_wd[:].bitcast(U16).rearrange("p (t m) -> p t m", t=PACK),
                        w_w[:].bitcast(U16).rearrange("p (m t) -> p t m", t=PACK))
         xt_wg = gather_packed("xt_wg", xt_w, l1, U32)
-        xt_sg = gather_packed("xt_sg", xt_s, l1, U8)
+        xt_sg = gather_packed("xt_sg", xt_s, l1, U8, slot="xt_w")
+        w_sd = deal_plane("w_sd", w_s)
         xo_wg = gather_packed("xo_wg", xo_w, l2, U32)
         xo_sg = gather_packed("xo_sg", xo_s, l2, U8)
-        w_sd = deal_plane("w_sd", w_s)
-        w2_wd = tile("w2_wd", [P, 2 * R], U8)
-        nc.gpsimd.tensor_copy(w2_wd[:].rearrange("p (t m b) -> p t m b", t=PACK, b=2),
-                              w2_w[:].rearrange("p (m t b) -> p t m b", t=PACK, b=2))
         w2_sd = deal_plane("w2_sd", w2_s)
+        w2_wd = tile("w2_wd", [P, 2 * R], U8)
+        nc.vector.tensor_copy(w2_wd[:].bitcast(U16).rearrange("p (t m) -> p t m", t=PACK),
+                              w2_w[:].bitcast(U16).rearrange("p (m t) -> p t m", t=PACK))
         a_ps = [psum.tile([P, J], F32, name="a_ps%d" % t) for t in range(PACK)]
-        a_sb = [tile("a_sb0", [P, J], F32), tile("a_sb1", [P, J], F32),
-                tile("a_sb2", [P, J], F32, slot="xo_s"), tile("a_sb3", [P, J], F32, slot="xo_w")]
+        a_late = tile("a_late", [P, 2, J], F32, slot="w2_w")
+        a_sb = [tile("a_sb0", [P, J], F32)[:], tile("a_sb1", [P, J], F32)[:], a_late[:, 0, :], a_late[:, 1, :]]
         for t in range(PACK):
             first_product(a_ps[t][:], t, w_wd, w_sd, xt_wg, xt_sg, E5M2)
         for t in (0, 1):
-            nc.scalar.copy(a_sb[t][:], a_ps[t][:])
+            nc.scalar.copy(a_sb[t], a_ps[t][:])
         for t in (2, 3):
-            nc.vector.tensor_copy(a_sb[t][:], a_ps[t][:])
+            nc.vector.tensor_copy(a_sb[t], a_ps[t][:])
         for t in (0, 1):
-            nc.scalar.activation(pw[t][:].indirect(l3[:]), a_sb[t][:], COPY)
+            nc.scalar.activation(pw[t][:].indirect(l3[:]), a_sb[t], COPY)
         for t in (2, 3):
-            nc.vector.tensor_copy(pw[t][:].indirect(l3[:]), a_sb[t][:])
+            nc.vector.tensor_copy(pw[t][:].indirect(l3[:]), a_sb[t])
 
         b_ps = [psum.tile([P, 2, J], F32, name="b_ps%d" % u) for u in range(2)]
         b_sb = [tile("b_sb%d" % u, [P, 2, J], F32) for u in range(2)]
@@ -136,14 +135,13 @@ def tile_list_readless_twotab_one_tabled_kernel(tc, xt_words, xt_scales, w_words
         bg = tile("bg", [P, PACK, O], F32)
         for u in range(2):
             nc.scalar.copy(b_sb[u][:], b_ps[u][:])
-        for t in (0, 1):
+        for t in (0, 1, 2):
             nc.scalar.activation(g5[:, t, :], pw[t][:].indirect(l5[:]), COPY)
         for t in range(PACK):
             nc.scalar.activation(bg[:, t, :], b_sb[t // 2][:, t % 2, :].indirect(l6[:]), COPY)
         for t in range(PACK):
             nc.vector.tensor_copy(g4[:, t, :], pw[t][:].indirect(l4[:]))
-        for t in (2, 3):
-            nc.vector.tensor_copy(g5[:, t, :], pw[t][:].indirect(l5[:]))
+        nc.vector.tensor_copy(g5[:, 3, :], pw[3][:].indirect(l5[:]))
         tzg = tile("tzg", [P, 2, O], F32, slot="b_sb1")
         for h in range(2):
             nc.scalar.activation(tzg[:, h, :], tzt[:, h, :].indirect(l7[:]), COPY)

from contextlib import ExitStack

import concourse.mybir as mybir

F32 = mybir.dt.float32
BF16 = mybir.dt.bfloat16
I32 = mybir.dt.int32
U32 = mybir.dt.uint32
U16 = mybir.dt.uint16
U8 = mybir.dt.uint8
E4M3 = mybir.dt.float8_e4m3fn_x4
E5M2 = mybir.dt.float8_e5m2_x4
E2M1 = mybir.dt.float4_e2m1fn_x4
ALU = mybir.AluOpType
COPY = mybir.ActivationFunctionType.Copy

P = 128
PACK = 4
T, Z, J, R, C, O, N, E = 1024, 1024, 256, 512, 512, 128, 256, 1024
FLOPS = 301989888


def tile_list_readless_twotab_one_tabled_kernel(tc, xt_words, xt_scales, w_words, w_scales, xo_words, xo_scales,
                                                     w2_words, w2_scales, wb_words, wb_scales, tz,
                                                     offs, offs2, offs3, offs4, offs5, offs6, offs7, out):
    nc = tc.nc
    with ExitStack() as ctx:
        sb = ctx.enter_context(tc.tile_pool(name="sb", bufs=1))
        psum = ctx.enter_context(tc.psum_pool(name="psum", bufs=1))

        def tile(name, shape, dtype, slot=None):
            return sb.tile(shape, dtype, name=name, tag=slot or name, align_bytes=64)

        def load_list(name, src):
            t = tile(name, [P, src.shape[1]], U16)
            nc.sync.dma_start(t[:], src)
            return t

        def load_words(name, src, dtype, cols, queue):
            t = tile(name, [P, cols], dtype)
            queue.dma_start(t[:].bitcast(I32), src.bitcast(I32))
            return t

        def plane_quadrant(t, src, q, queue):
            queue.dma_start(t[32 * q : 32 * q + 4, :].bitcast(I32), src[0, 4 * q : 4 * q + 4, :].bitcast(I32))

        def plane_head(t, src, queue):
            queue.dma_start(t[0:2, :].bitcast(I32), src[0, 0:2, :].bitcast(I32))

        def plane_rest(t, src, queue):
            rows = src[0, 2:16, :].bitcast(I32)
            queue.dma_start(t[2:P, :].bitcast(I32), rows.unsqueeze(0).broadcast_to([9, 14, src.shape[2] // 4]))

        xt_s = tile("xt_s", [P, T], U8)
        w_s = tile("w_s", [P, R], U8)
        xo_s = tile("xo_s", [P, Z], U8)
        w2_s = tile("w2_s", [P, R], U8)
        wb_s = tile("wb_s", [P, N], U8)
        tzt = tile("tzt", [P, 2, E], F32)
        pw = [tile("pw%d" % t, [P, C], F32) for t in range(PACK)]
        for t in range(PACK):
            nc.gpsimd.memset(pw[t][:], 0.0)

        plane_head(xt_s, xt_scales, nc.scalar)
        l1 = load_list("l1", offs)
        xt_w = load_words("xt_w", xt_words[0].rearrange("p c t -> p (c t)"), U32, T, nc.sync)
        plane_rest(xt_s, xt_scales, nc.scalar)
        w_w = load_words("w_w", w_words[0], U8, 2 * R, nc.scalar)
        plane_head(w_s, w_scales, nc.sync)
        plane_rest(w_s, w_scales, nc.sync)
        xo_w = load_words("xo_w", xo_words[0].rearrange("p c t -> p (c t)"), U32, Z, nc.sync)
        l2 = load_list("l2", offs2)
        plane_rest(xo_s, xo_scales, nc.sync)
        plane_head(xo_s, xo_scales, nc.sync)
        l3 = load_list("l3", offs3)
        plane_rest(w2_s, w2_scales, nc.sync)
        plane_head(w2_s, w2_scales, nc.sync)
        w2_w = load_words("w2_w", w2_words[0], U8, 2 * R, nc.sync)
        l5 = load_list("l5", offs5)
        l4 = load_list("l4", offs4)
        l6 = load_list("l6", offs6)
        nc.sync.dma_start(tzt[:], tz.rearrange("(h p) e -> p h e", p=P))
        l7 = load_list("l7", offs7)
        wb_w = load_words("wb_w", wb_words[0], U8, 2 * N, nc.sync)
        plane_head(wb_s, wb_scales, nc.sync)
        plane_rest(wb_s, wb_scales, nc.sync)

        def deal_plane(name, src):
            t = tile(name, [P, R], U8)
            nc.vector.tensor_copy(t[:].rearrange("p (t m) -> p t m", t=PACK), src[:].rearrange("p (m t) -> p t m", t=PACK))
            return t

        def gather_packed(name, src, lst, dtype, slot=None):
            t = tile(name, [P, J], dtype, slot)
            nc.vector.tensor_copy(t[:], src[:].indirect(lst[:]))
            return t

        def first_product(bank, t, ww, ws, xw, xs, fmt):
            nc.tensor.matmul_mx(out=bank, lhsT=ww[:, 2 * P * t : 2 * P * (t + 1)].bitcast(E2M1),
                                lhsT_scale=ws[:, P * t : P * (t + 1)], rhs=xw[:].bitcast(fmt), rhs_scale=xs[:],
                                start=True, stop=True)

        w_wd = tile("w_wd", [P, 2 * R], U8)
        nc.scalar.copy(w_wd[:].bitcast(U16).rearrange("p (t m) -> p t m", t=PACK),
                       w_w[:].bitcast(U16).rearrange("p (m t) -> p t m", t=PACK))
        xt_wg = gather_packed("xt_wg", xt_w, l1, U32)
        xt_sg = gather_packed("xt_sg", xt_s, l1, U8, slot="xt_w")
        w_sd = deal_plane("w_sd", w_s)
        xo_wg = gather_packed("xo_wg", xo_w, l2, U32)
        xo_sg = gather_packed("xo_sg", xo_s, l2, U8)
        w2_sd = deal_plane("w2_sd", w2_s)
        w2_wd = tile("w2_wd", [P, 2 * R], U8)
        nc.vector.tensor_copy(w2_wd[:].bitcast(U16).rearrange("p (t m) -> p t m", t=PACK),
                              w2_w[:].bitcast(U16).rearrange("p (m t) -> p t m", t=PACK))
        a_ps = [psum.tile([P, J], F32, name="a_ps%d" % t) for t in range(PACK)]
        a_late = tile("a_late", [P, 2, J], F32, slot="w2_w")
        a_sb = [tile("a_sb0", [P, J], F32)[:], tile("a_sb1", [P, J], F32)[:], a_late[:, 0, :], a_late[:, 1, :]]
        for t in range(PACK):
            first_product(a_ps[t][:], t, w_wd, w_sd, xt_wg, xt_sg, E5M2)
        for t in (0, 1):
            nc.scalar.copy(a_sb[t], a_ps[t][:])
        for t in (2, 3):
            nc.vector.tensor_copy(a_sb[t], a_ps[t][:])
        for t in (0, 1):
            nc.scalar.activation(pw[t][:].indirect(l3[:]), a_sb[t], COPY)
        for t in (2, 3):
            nc.vector.tensor_copy(pw[t][:].indirect(l3[:]), a_sb[t])

        b_ps = [psum.tile([P, 2, J], F32, name="b_ps%d" % u) for u in range(2)]
        b_sb = [tile("b_sb%d" % u, [P, 2, J], F32) for u in range(2)]
        for t in range(PACK):
            first_product(b_ps[t // 2][:, t % 2, :], t, w2_wd, w2_sd, xo_wg, xo_sg, E4M3)
        g4 = tile("g4", [P, PACK, O], F32)
        g5 = tile("g5", [P, PACK, O], F32)
        bg = tile("bg", [P, PACK, O], F32)
        for u in range(2):
            nc.scalar.copy(b_sb[u][:], b_ps[u][:])
        for t in (0, 1, 2):
            nc.scalar.activation(g5[:, t, :], pw[t][:].indirect(l5[:]), COPY)
        for t in range(PACK):
            nc.scalar.activation(bg[:, t, :], b_sb[t // 2][:, t % 2, :].indirect(l6[:]), COPY)
        for t in range(PACK):
            nc.vector.tensor_copy(g4[:, t, :], pw[t][:].indirect(l4[:]))
        nc.vector.tensor_copy(g5[:, 3, :], pw[3][:].indirect(l5[:]))
        tzg = tile("tzg", [P, 2, O], F32, slot="b_sb1")
        for h in range(2):
            nc.scalar.activation(tzg[:, h, :], tzt[:, h, :].indirect(l7[:]), COPY)

        top = tile("top", [P, PACK, O], F32)
        hid = tile("hid", [P, O * PACK], BF16)
        hid_w = tile("hid_w", [P, O], U32)
        hid_s = tile("hid_s", [P, O], U8)
        halves = [slice(0, O // 2), slice(O // 2, O)]
        for o in halves:
            nc.vector.tensor_tensor(top[:, :, o], g4[:, :, o], g5[:, :, o], ALU.max)
        for o in halves:
            nc.vector.tensor_tensor(hid[:, PACK * o.start : PACK * o.stop].rearrange("p (c i t) -> p c t i", i=4, t=PACK),
                                    top[:, :, o].rearrange("p t (c i) -> p c t i", i=4),
                                    bg[:, :, o].rearrange("p t (c i) -> p c t i", i=4), ALU.subtract)
        for o in halves:
            nc.vector.quantize_mx(out=hid_w[:, o].bitcast(E4M3), scales=hid_s[:, o], in_=hid[:, PACK * o.start : PACK * o.stop])
        for h in range(2):
            p_ps = psum.tile([P, O], F32, name="p_ps%d" % h)
            nc.tensor.matmul_mx(out=p_ps[:], lhsT=wb_w[:, 2 * P * h : 2 * P * (h + 1)].bitcast(E2M1),
                                lhsT_scale=wb_s[:, P * h : P * (h + 1)], rhs=hid_w[:].bitcast(E4M3), rhs_scale=hid_s[:],
                                start=True, stop=True)
            res = tile("res%d" % h, [P, O], F32)
            nc.vector.tensor_tensor(res[:], p_ps[:], tzg[:, h, :], ALU.add)
            (nc.sync if h == 0 else nc.scalar).dma_start(out[P * h : P * (h + 1), :], res[:])
